import numpy as np
import ml_dtypes


def mxq(x, axis, fmt="e4m3"):
    dtype, down = {"e4m3": (ml_dtypes.float8_e4m3fn, 7), "e5m2": (ml_dtypes.float8_e5m2, 14)}[fmt]
    v = np.moveaxis(np.asarray(x, np.float32).astype(ml_dtypes.bfloat16).astype(np.float64), axis, -1)
    blocks = v.reshape(v.shape[:-1] + (-1, 32))
    amax = np.abs(blocks).max(-1, keepdims=True)
    byte = np.maximum(np.where(amax > 0, np.frexp(amax)[1] - 1 + 127, 0) - down, 1)
    scale = np.exp2(byte - 127.0)
    codes = (blocks / scale).astype(np.float32).astype(dtype).astype(np.float64)
    return np.moveaxis((codes * scale).reshape(v.shape), -1, axis)


WIDE = False


def mx_kscale(k):
    if not WIDE:
        return np.ones(k)
    levels = np.array([10, -10, 5, -5, 0])
    if k % 512:
        return np.exp2(np.random.permutation(np.resize(levels, k // 32))).repeat(32)
    a = np.empty((k // 512, 16))
    for p in range(k // 512):
        a[p, :8] = np.random.permutation(np.resize(levels, 8))
        for g in range(8):
            far = levels[np.abs(levels - a[p, g]) >= 10]
            a[p, g + 8] = far[np.random.randint(len(far))]
    return np.exp2(a.ravel()).repeat(32)


def f64(x):
    return np.asarray(x).astype(np.float64)


def striped(idx):
    return np.tile(idx.reshape(-1, 16).T, (8, 1)).astype(np.uint16)


def unstriped(offs):
    return offs[:16].T.reshape(-1).astype(np.int64)


def striped8(idx):
    return np.concatenate([x.reshape(-1, 16).T for x in idx]).astype(np.uint16)


def runs(offs, k):
    lists = np.stack([offs[16 * r : 16 * r + 16].T.reshape(-1) for r in range(8)]).astype(np.int64)
    return lists[np.arange(k) % 512 // 64]


def pack_weight(w):
    k, n = w.shape
    w = f64(np.asarray(w, np.float32).astype(ml_dtypes.bfloat16)).reshape(k // 32, 32, n)
    amax = np.abs(w).max(1)
    byte = np.clip(np.where(amax > 0, np.frexp(amax)[1] - 1 + 127 - 7, 1), 1, 254)
    scaled = (w * np.exp2(127.0 - byte)[:, None, :]).reshape(k, n).astype(np.float32)
    words = np.ascontiguousarray(scaled.reshape(k // 512, 128, 4, n).transpose(0, 1, 3, 2)).astype(ml_dtypes.float8_e4m3fn).view(np.uint8)
    return words, np.ascontiguousarray(byte.astype(np.uint8).reshape(k // 512, 16, n))


def unpack_weight(words, scales):
    g, p, n, _ = words.shape
    vals = np.ascontiguousarray(words).view(ml_dtypes.float8_e4m3fn).astype(np.float64) * np.repeat(np.exp2(scales.astype(np.float64) - 127.0), 8, axis=1)[..., None]
    return vals.transpose(0, 1, 3, 2).reshape(g * 512, n)


def sigmoid(v):
    return 1.0 / (1.0 + np.exp(-np.maximum(v, -700.0)))


K, T, S, H, W, G = 512, 1024, 256, 512, 128, 2048


def setup_inputs():
    n = np.random.standard_normal
    s = mx_kscale(K)[:, None]
    packed_xT = pack_weight(n((K, T)) * s)
    packed_dT = pack_weight(n((K, G)) / s)
    perm = np.random.permutation(S)
    perm2 = np.random.permutation(S)
    perm3 = np.random.permutation(S)
    return {
        "x_words": packed_xT[0],
        "x_scales": packed_xT[1],
        "w1": (n((K, H)) / np.sqrt(2 * K) / s).astype(np.float32),
        "w2": (n((K, H)) / np.sqrt(2 * K) / s).astype(np.float32),
        "gs": (np.random.uniform(0.5, 1.5, (K, 1)) * s).astype(np.float32),
        "d_words": packed_dT[0],
        "d_scales": packed_dT[1],
        "sl": np.random.uniform(1.0, 2.0, (H, 1)).astype(np.float32),
        "th": (0.5 * n((H, 1))).astype(np.float32),
        "offs": striped8(np.random.randint(0, T, (8, S))),
        "hz": striped8(np.random.randint(0, T, (8, S))),
        "n1": striped(perm[:W]),
        "n2": striped(perm[W:]),
        "k1": striped8(np.random.randint(0, G, (8, H))),
        "k2": striped8(np.random.randint(0, G, (8, H))),
        "two": striped(np.random.permutation(T)[:S]),
        "k3": striped8(np.random.randint(0, G, (8, H))),
        "hy": striped8(np.random.randint(0, T, (8, S))),
        "n3": striped(np.random.permutation(S)),
        "n4": striped(perm2[:W]),
        "n5": striped(perm2[W:]),
        "n6": striped(perm3[:W]),
        "n7": striped(perm3[W:]),
    }


def reference(x_words, x_scales, w1, w2, gs, d_words, d_scales, sl, th, offs, hz, n1, n2, k1, k2, two, k3, hy, n3, n4, n5, n6, n7):
    d_k1 = unpack_weight(d_words, d_scales)[np.arange(K)[:, None], runs(k1, K)]
    xq = unpack_weight(x_words, x_scales)[np.arange(K)[:, None], runs(offs, K)]
    x_hz = unpack_weight(x_words, x_scales)[np.arange(K)[:, None], runs(hz, K)]
    y = mxq(f64(w1), 0, "e4m3").T @ xq + mxq(f64(w2), 0, "e4m3").T @ x_hz
    pb = y[:, unstriped(n2)]
    pa = y[:, unstriped(n1)]
    rb = pb - (0.5 * pa)
    ra = np.sqrt((pa) ** 2 + (pb) ** 2 + 0.25)
    ua = np.zeros((H, S))
    ua[:, unstriped(n1)] = ra
    ub = ua.copy()
    ub[:, unstriped(n2)] = rb
    z = f64(gs) * ub
    d_k2 = unpack_weight(d_words, d_scales)[np.arange(K)[:, None], runs(k2, K)]
    x_two = unpack_weight(x_words, x_scales)[:, unstriped(two)]
    d_k3 = unpack_weight(d_words, d_scales)[np.arange(K)[:, None], runs(k3, K)]
    x_hy = unpack_weight(x_words, x_scales)[np.arange(K)[:, None], runs(hy, K)]
    h2 = 0.0625 * ((d_k1.T @ mxq(z, 0, "e4m3") + d_k2.T @ x_two + d_k3.T @ x_hy))
    sg = sigmoid(f64(sl) * (h2[:, unstriped(n3)] - f64(th)))
    st = h2 * sg
    pa2 = st[:, unstriped(n4)]
    pb2 = st[:, unstriped(n5)]
    rb2 = pa2 - pb2
    ra2 = np.maximum(pa2, pb2)
    ua2 = np.zeros((H, S))
    ua2[:, unstriped(n6)] = ra2
    out = ua2.copy()
    out[:, unstriped(n7)] = rb2
    return out

@@ -1,0 +1,216 @@
+from contextlib import ExitStack
+
+import concourse.mybir as mybir
+
+K, T, S, H, W, G = 512, 1024, 256, 512, 128, 2048
+FLOPS = 5 * 2 * K * H * S
+
+F32 = mybir.dt.float32
+BF16 = mybir.dt.bfloat16
+I32 = mybir.dt.int32
+U32 = mybir.dt.uint32
+U16 = mybir.dt.uint16
+U8 = mybir.dt.uint8
+FP8X4 = mybir.dt.float8_e4m3fn_x4
+ALU = mybir.AluOpType
+ACT = mybir.ActivationFunctionType
+
+P = 128
+PACK = 4
+TILES = H // P
+SPLIT = 80
+
+
+def tile_picked_dhhzmthpolarecpx_none_p_kernel(
+    tc, x_words, x_scales, w1, w2, gs, d_words, d_scales, sl, th,
+    offs, hz, n1, n2, k1, k2, two, k3, hy, n3, n4, n5, n6, n7, out,
+):
+    nc = tc.nc
+    with ExitStack() as ctx:
+        keep = ctx.enter_context(tc.tile_pool(name="keep", bufs=1))
+        psum = ctx.enter_context(tc.psum_pool(name="psum", bufs=1))
+
+        def new(name, shape, dtype):
+            return keep.tile(shape, dtype, name=name, align_bytes=64)
+
+        def load_list(name, src):
+            lst = new("list_" + name, list(src.shape), U16)
+            nc.sync.dma_start(lst[:], src)
+            return lst
+
+        def scale_window(name, width):
+            window = new(name, [P, width], U8)
+            nc.gpsimd.memset(window[:].bitcast(I32), 0)
+            return window
+
+        def load_scale_rows(window, scales, queue):
+            for i in range(2):
+                queue.dma_start(window[i:P:16, :].bitcast(I32), scales[0, i:16:2, :].bitcast(I32))
+
+        def load_words(name, words, width):
+            window = new(name, [P, width], I32)
+            nc.sync.dma_start(window[:], words[0].rearrange("p n t -> p (n t)").bitcast(I32))
+            return window
+
+        def load_weight(name, w):
+            rows = new(name, [P, PACK, H], F32)
+            nc.sync.dma_start(rows[:], w.rearrange("(p j) c -> p j c", j=PACK))
+            return rows
+
+        def place_scales(name, picked, width, queue):
+            plane = new(name, [P, width], U8)
+            nc.vector.tensor_copy(plane[:].bitcast(I32), picked[:].bitcast(I32))
+            for i in range(2):
+                queue.dma_start(plane[2 + i:P:32, :].bitcast(I32), picked[16 + i:P:32, :].bitcast(I32))
+            return plane
+
+        def gather_words(dst, window, offsets):
+            nc.vector.tensor_copy(dst, window[:].bitcast(U32).indirect(offsets))
+
+        x_byte_win = scale_window("x_byte_win", T)
+        d_byte_win = scale_window("d_byte_win", G)
+        quarter = new("quarter", [P, 1], F32)
+        nc.gpsimd.memset(quarter[:], 0.25)
+        load_scale_rows(x_byte_win, x_scales, nc.scalar)
+        l_offs = load_list("offs", offs)
+        l_hz = load_list("hz", hz)
+        l_two = load_list("two", two)
+        l_hy = load_list("hy", hy)
+        raw = [load_weight("w1_raw", w1)]
+        x_word_win = load_words("x_word_win", x_words, T)
+        raw.append(load_weight("w2_raw", w2))
+        l1 = load_list("n1", n1)
+        l2 = load_list("n2", n2)
+        load_scale_rows(d_byte_win, d_scales, nc.sync)
+        d_lists = [load_list(name, src) for name, src in (("k1", k1), ("k2", k2), ("k3", k3))]
+        d_word_win = load_words("d_word_win", d_words, G)
+        gain = new("gain", [P, PACK], F32)
+        nc.sync.dma_start(gain[:], gs.rearrange("(p t) o -> p (t o)", t=PACK))
+        l3, l4, l5, l6, l7 = [load_list(name, src) for name, src in (("n3", n3), ("n4", n4), ("n5", n5), ("n6", n6), ("n7", n7))]
+        slope = new("slope", [P, TILES], F32)
+        thresh = new("thresh", [P, TILES], F32)
+        with nc.allow_non_contiguous_dma(reason="one value a row"):
+            nc.sync.dma_start(slope[:], sl.rearrange("(i p) o -> p (i o)", p=P))
+            nc.sync.dma_start(thresh[:], th.rearrange("(i p) o -> p (i o)", p=P))
+
+        x_bytes = new("x_bytes", [P, 2 * S], U8)
+        for a, lst in enumerate((l_offs, l_hz)):
+            nc.vector.tensor_copy(x_bytes[:, a * S:(a + 1) * S], x_byte_win[:].indirect(lst[:]))
+        x_plane = place_scales("x_plane", x_bytes, 2 * S, nc.scalar)
+        x_picked = []
+        for a, lst in enumerate((l_offs, l_hz)):
+            words = new("x_picked%d" % a, [P, S], U32)
+            gather_words(words[:], x_word_win, lst[:])
+            x_picked.append(words)
+        late_bytes = new("late_bytes", [P, 2 * S + 3 * H], U8)
+        for a, lst in enumerate((l_two, l_hy)):
+            nc.vector.tensor_copy(late_bytes[:, a * S:(a + 1) * S], x_byte_win[:].indirect(lst[:]))
+
+        grouped = [keep.tile([P, PACK * H], BF16, name="w_grouped%d" % a, tag="w_grouped%d" % a, align_bytes=64) for a in range(2)]
+        dst = [grouped[a][:].rearrange("p (t m j) -> p m j t", t=TILES, j=PACK) for a in range(2)]
+        src = [raw[a][:].rearrange("p j (m t) -> p m j t", t=TILES) for a in range(2)]
+        nc.scalar.copy(dst[0], src[0])
+        nc.vector.tensor_copy(dst[1][:, :SPLIT], src[1][:, :SPLIT])
+        nc.scalar.copy(dst[1][:, SPLIT:], src[1][:, SPLIT:])
+        w_codes = [new("w_codes%d" % a, [P, H], U32) for a in range(2)]
+        w_plane = [new("w_plane%d" % a, [P, H], U8) for a in range(2)]
+
+        y = []
+        for t in range(TILES):
+            cols = slice(t * P, (t + 1) * P)
+            acc = psum.tile([P, S], F32, name="y_acc%d" % t)
+            for a in range(2):
+                nc.vector.quantize_mx(
+                    out=w_codes[a][:, cols].bitcast(FP8X4), scales=w_plane[a][:, cols],
+                    in_=grouped[a][:, t * PACK * P:(t + 1) * PACK * P])
+            for a in range(2):
+                nc.tensor.matmul_mx(
+                    out=acc[:], lhsT=w_codes[a][:, cols].bitcast(FP8X4), lhsT_scale=w_plane[a][:, cols],
+                    rhs=x_picked[a][:].bitcast(FP8X4), rhs_scale=x_plane[:, a * S:(a + 1) * S],
+                    start=(a == 0), stop=(a == 1))
+            y_t = new("y%d" % t, [P, S], F32)
+            nc.vector.tensor_copy(y_t[:], acc[:])
+            y.append(y_t)
+
+        z_grouped = new("z_grouped", [P, S, PACK], BF16)
+        pairs = []
+        for t in range(TILES):
+            pair = new("pair%d" % t, [P, S], F32)
+            nc.scalar.activation(pair[:, :W], y[t][:].indirect(l1[:]), ACT.Copy)
+            nc.scalar.activation(pair[:, W:], y[t][:].indirect(l2[:]), ACT.Copy)
+            pairs.append(pair)
+        for t in range(TILES):
+            pair = pairs[t]
+            rb = new("rb%d" % t, [P, W], F32)
+            sq = new("sq%d" % t, [P, S], F32)
+            ssum = new("ssum%d" % t, [P, W], F32)
+            ra = new("ra%d" % t, [P, W], F32)
+            ub = new("ub%d" % t, [P, S], F32)
+            nc.gpsimd.tensor_tensor(sq[:], pair[:], pair[:], ALU.mult)
+            nc.vector.scalar_tensor_tensor(rb[:], pair[:, :W], -0.5, pair[:, W:], ALU.mult, ALU.add)
+            nc.gpsimd.tensor_tensor(ssum[:], sq[:, :W], sq[:, W:], ALU.add)
+            nc.scalar.activation(ub[:].indirect(l2[:]), rb[:], ACT.Copy)
+            nc.scalar.activation(ra[:], ssum[:], ACT.Sqrt, bias=quarter[:])
+            nc.scalar.activation(ub[:].indirect(l1[:]), ra[:], ACT.Copy)
+            nc.vector.tensor_scalar(z_grouped[:, :, t], ub[:], gain[:, t:t + 1], None, ALU.mult)
+
+        for a, lst in enumerate(d_lists):
+            for h in range(2):
+                at = 2 * S + a * H + h * S
+                nc.vector.tensor_copy(late_bytes[:, at:at + S], d_byte_win[:].indirect(lst[:, 16 * h:16 * (h + 1)]))
+        late_plane = place_scales("late_plane", late_bytes, 2 * S + 3 * H, nc.sync)
+        x_late = keep.tile([P, 2, S], U32, name="x_late", tag="w_grouped1", align_bytes=64)
+        for a, lst in enumerate((l_two, l_hy)):
+            gather_words(x_late[:, a, :], x_word_win, lst[:])
+
+        def pick_codewords(h):
+            words = keep.tile([P, 3, S], U32, name="d_picked%d" % h, tag="d_picked", align_bytes=64)
+            for a, lst in enumerate(d_lists):
+                gather_words(words[:, a, :], d_word_win, lst[:, 16 * h:16 * (h + 1)])
+            return words
+
+        d_picked = pick_codewords(0)
+        z_codes = new("z_codes", [P, S], U32)
+        z_plane = new("z_plane", [P, S], U8)
+        nc.vector.quantize_mx(out=z_codes[:].bitcast(FP8X4), scales=z_plane[:], in_=z_grouped[:].rearrange("p c t -> p (c t)"))
+        bias = new("bias", [P, TILES], F32)
+        nc.vector.scalar_tensor_tensor(bias[:], slope[:], -1.0, thresh[:], ALU.mult, ALU.mult)
+
+        moving = [
+            (1, x_late[:, 0, :], late_plane[:, 0:S]),
+            (2, x_late[:, 1, :], late_plane[:, S:2 * S]),
+            (0, z_codes[:], z_plane[:]),
+        ]
+        h2 = []
+        for i in range(TILES):
+            if i == 2:
+                d_picked = pick_codewords(1)
+            acc = psum.tile([P, S], F32, name="h_acc%d" % i)
+            for n, (a, codes, plane) in enumerate(moving):
+                nc.tensor.matmul_mx(
+                    out=acc[:],
+                    lhsT=d_picked[:, a, (i % 2) * P:(i % 2 + 1) * P].bitcast(FP8X4),
+                    lhsT_scale=late_plane[:, 2 * S + a * H + i * P:2 * S + a * H + (i + 1) * P],
+                    rhs=codes.bitcast(FP8X4), rhs_scale=plane,
+                    start=(n == 0), stop=(n == 2))
+            h_i = new("h%d" % i, [P, S], F32)
+            nc.vector.tensor_scalar(h_i[:], acc[:], 0.0625, None, ALU.mult)
+            h2.append(h_i)
+        for i in range(TILES):
+            sg = new("sg%d" % i, [P, S], F32)
+            st = new("st%d" % i, [P, S], F32)
+            pair = new("pair2_%d" % i, [P, S], F32)
+            big = new("big%d" % i, [P, W], F32)
+            diff = new("diff%d" % i, [P, W], F32)
+            res = new("res%d" % i, [P, S], F32)
+            for h in range(2):
+                nc.scalar.activation(sg[:, h * W:(h + 1) * W], h2[i][:].indirect(l3[:, 8 * h:8 * (h + 1)]), ACT.Sigmoid,
+                                     bias=bias[:, i:i + 1], scale=slope[:, i:i + 1])
+            nc.vector.tensor_tensor(st[:], h2[i][:], sg[:], ALU.mult)
+            nc.scalar.activation(pair[:, :W], st[:].indirect(l4[:]), ACT.Copy)
+            nc.scalar.activation(pair[:, W:], st[:].indirect(l5[:]), ACT.Copy)
+            nc.vector.tensor_tensor(big[:], pair[:, :W], pair[:, W:], ALU.max)
+            nc.vector.tensor_tensor(diff[:], pair[:, :W], pair[:, W:], ALU.subtract)
+            nc.scalar.activation(res[:].indirect(l6[:]), big[:], ACT.Copy)
+            nc.scalar.activation(res[:].indirect(l7[:]), diff[:], ACT.Copy)
+            nc.sync.dma_start(out[i * P:(i + 1) * P, :], res[:])

@@ -18,7 +18,7 @@ ACT = mybir.ActivationFunctionType
 P = 128
 PACK = 4
 TILES = H // P
-SPLIT = 80
+SPLIT = (32, 72)
 
 
 def tile_picked_dhhzmthpolarecpx_none_p_kernel(
@@ -38,14 +38,11 @@ def tile_picked_dhhzmthpolarecpx_none_p_kernel(
             nc.sync.dma_start(lst[:], src)
             return lst
 
-        def scale_window(name, width):
+        def load_scale_rows(name, scales, width):
             window = new(name, [P, width], U8)
-            nc.gpsimd.memset(window[:].bitcast(I32), 0)
+            rows = scales[0].bitcast(I32).unsqueeze(1).broadcast_to([16, 8, width // 4])
+            nc.sync.dma_start(window[:].bitcast(I32), rows)
             return window
-
-        def load_scale_rows(window, scales, queue):
-            for i in range(2):
-                queue.dma_start(window[i:P:16, :].bitcast(I32), scales[0, i:16:2, :].bitcast(I32))
 
         def load_words(name, words, width):
             window = new(name, [P, width], I32)
@@ -60,28 +57,27 @@ def tile_picked_dhhzmthpolarecpx_none_p_kernel(
         def place_scales(name, picked, width, queue):
             plane = new(name, [P, width], U8)
             nc.vector.tensor_copy(plane[:].bitcast(I32), picked[:].bitcast(I32))
-            for i in range(2):
-                queue.dma_start(plane[2 + i:P:32, :].bitcast(I32), picked[16 + i:P:32, :].bitcast(I32))
+            for j in range(1, 4):
+                queue.dma_start(plane[j:P:32, :].bitcast(I32), picked[8 * j:P:32, :].bitcast(I32))
             return plane
 
         def gather_words(dst, window, offsets):
             nc.vector.tensor_copy(dst, window[:].bitcast(U32).indirect(offsets))
 
-        x_byte_win = scale_window("x_byte_win", T)
-        d_byte_win = scale_window("d_byte_win", G)
         quarter = new("quarter", [P, 1], F32)
         nc.gpsimd.memset(quarter[:], 0.25)
-        load_scale_rows(x_byte_win, x_scales, nc.scalar)
+        warm = new("warm", [P, 1], F32)
+        nc.scalar.activation(warm[:], quarter[:], ACT.Sqrt, bias=quarter[:])
+        x_byte_win = load_scale_rows("x_byte_win", x_scales, T)
         l_offs = load_list("offs", offs)
         l_hz = load_list("hz", hz)
         l_two = load_list("two", two)
         l_hy = load_list("hy", hy)
-        raw = [load_weight("w1_raw", w1)]
         x_word_win = load_words("x_word_win", x_words, T)
-        raw.append(load_weight("w2_raw", w2))
+        raw = [load_weight("w1_raw", w1), load_weight("w2_raw", w2)]
         l1 = load_list("n1", n1)
         l2 = load_list("n2", n2)
-        load_scale_rows(d_byte_win, d_scales, nc.sync)
+        d_byte_win = load_scale_rows("d_byte_win", d_scales, G)
         d_lists = [load_list(name, src) for name, src in (("k1", k1), ("k2", k2), ("k3", k3))]
         d_word_win = load_words("d_word_win", d_words, G)
         gain = new("gain", [P, PACK], F32)
@@ -98,7 +94,7 @@ def tile_picked_dhhzmthpolarecpx_none_p_kernel(
             nc.vector.tensor_copy(x_bytes[:, a * S:(a + 1) * S], x_byte_win[:].indirect(lst[:]))
         x_plane = place_scales("x_plane", x_bytes, 2 * S, nc.scalar)
         x_picked = []
-        for a, lst in enumerate((l_offs, l_hz)):
+        for a, lst in enumerate((l_offs, l_hz, l_two, l_hy)):
             words = new("x_picked%d" % a, [P, S], U32)
             gather_words(words[:], x_word_win, lst[:])
             x_picked.append(words)
@@ -109,9 +105,9 @@ def tile_picked_dhhzmthpolarecpx_none_p_kernel(
         grouped = [keep.tile([P, PACK * H], BF16, name="w_grouped%d" % a, tag="w_grouped%d" % a, align_bytes=64) for a in range(2)]
         dst = [grouped[a][:].rearrange("p (t m j) -> p m j t", t=TILES, j=PACK) for a in range(2)]
         src = [raw[a][:].rearrange("p j (m t) -> p m j t", t=TILES) for a in range(2)]
-        nc.scalar.copy(dst[0], src[0])
-        nc.vector.tensor_copy(dst[1][:, :SPLIT], src[1][:, :SPLIT])
-        nc.scalar.copy(dst[1][:, SPLIT:], src[1][:, SPLIT:])
+        for a in range(2):
+            nc.vector.tensor_copy(dst[a][:, :SPLIT[a]], src[a][:, :SPLIT[a]])
+            nc.scalar.copy(dst[a][:, SPLIT[a]:], src[a][:, SPLIT[a]:])
         w_codes = [new("w_codes%d" % a, [P, H], U32) for a in range(2)]
         w_plane = [new("w_plane%d" % a, [P, H], U8) for a in range(2)]
 
@@ -119,17 +115,22 @@ def tile_picked_dhhzmthpolarecpx_none_p_kernel(
         for t in range(TILES):
             cols = slice(t * P, (t + 1) * P)
             acc = psum.tile([P, S], F32, name="y_acc%d" % t)
-            for a in range(2):
-                nc.vector.quantize_mx(
-                    out=w_codes[a][:, cols].bitcast(FP8X4), scales=w_plane[a][:, cols],
-                    in_=grouped[a][:, t * PACK * P:(t + 1) * PACK * P])
+            if t < 3:
+                lo, hi = t * P, (t + 1) * P if t < 2 else H
+                for a in range(2):
+                    nc.vector.quantize_mx(
+                        out=w_codes[a][:, lo:hi].bitcast(FP8X4), scales=w_plane[a][:, lo:hi],
+                        in_=grouped[a][:, PACK * lo:PACK * hi])
             for a in range(2):
                 nc.tensor.matmul_mx(
                     out=acc[:], lhsT=w_codes[a][:, cols].bitcast(FP8X4), lhsT_scale=w_plane[a][:, cols],
                     rhs=x_picked[a][:].bitcast(FP8X4), rhs_scale=x_plane[:, a * S:(a + 1) * S],
                     start=(a == 0), stop=(a == 1))
             y_t = new("y%d" % t, [P, S], F32)
-            nc.vector.tensor_copy(y_t[:], acc[:])
+            if t == 0:
+                nc.scalar.copy(y_t[:], acc[:])
+            else:
+                nc.vector.tensor_copy(y_t[:], acc[:])
             y.append(y_t)
 
         z_grouped = new("z_grouped", [P, S, PACK], BF16)
@@ -146,8 +147,9 @@ def tile_picked_dhhzmthpolarecpx_none_p_kernel(
             ssum = new("ssum%d" % t, [P, W], F32)
             ra = new("ra%d" % t, [P, W], F32)
             ub = new("ub%d" % t, [P, S], F32)
+            nc.gpsimd.tensor_scalar(ssum[:], pair[:, :W], -0.5, 0.0, ALU.mult, ALU.add)
+            nc.gpsimd.tensor_tensor(rb[:], ssum[:], pair[:, W:], ALU.add)
             nc.gpsimd.tensor_tensor(sq[:], pair[:], pair[:], ALU.mult)
-            nc.vector.scalar_tensor_tensor(rb[:], pair[:, :W], -0.5, pair[:, W:], ALU.mult, ALU.add)
             nc.gpsimd.tensor_tensor(ssum[:], sq[:, :W], sq[:, W:], ALU.add)
             nc.scalar.activation(ub[:].indirect(l2[:]), rb[:], ACT.Copy)
             nc.scalar.activation(ra[:], ssum[:], ACT.Sqrt, bias=quarter[:])
@@ -155,21 +157,17 @@ def tile_picked_dhhzmthpolarecpx_none_p_kernel(
             nc.vector.tensor_scalar(z_grouped[:, :, t], ub[:], gain[:, t:t + 1], None, ALU.mult)
 
         for a, lst in enumerate(d_lists):
-            for h in range(2):
-                at = 2 * S + a * H + h * S
-                nc.vector.tensor_copy(late_bytes[:, at:at + S], d_byte_win[:].indirect(lst[:, 16 * h:16 * (h + 1)]))
+            at = 2 * S + a * H
+            nc.vector.tensor_copy(late_bytes[:, at:at + H], d_byte_win[:].indirect(lst[:]))
         late_plane = place_scales("late_plane", late_bytes, 2 * S + 3 * H, nc.sync)
-        x_late = keep.tile([P, 2, S], U32, name="x_late", tag="w_grouped1", align_bytes=64)
-        for a, lst in enumerate((l_two, l_hy)):
-            gather_words(x_late[:, a, :], x_word_win, lst[:])
 
         def pick_codewords(h):
-            words = keep.tile([P, 3, S], U32, name="d_picked%d" % h, tag="d_picked", align_bytes=64)
+            words = keep.tile([P, 3, S], U32, name="d_picked%d" % h, align_bytes=64)
             for a, lst in enumerate(d_lists):
                 gather_words(words[:, a, :], d_word_win, lst[:, 16 * h:16 * (h + 1)])
             return words
 
-        d_picked = pick_codewords(0)
+        d_picked = [pick_codewords(h) for h in range(2)]
         z_codes = new("z_codes", [P, S], U32)
         z_plane = new("z_plane", [P, S], U8)
         nc.vector.quantize_mx(out=z_codes[:].bitcast(FP8X4), scales=z_plane[:], in_=z_grouped[:].rearrange("p c t -> p (c t)"))
@@ -177,19 +175,17 @@ def tile_picked_dhhzmthpolarecpx_none_p_kernel(
         nc.vector.scalar_tensor_tensor(bias[:], slope[:], -1.0, thresh[:], ALU.mult, ALU.mult)
 
         moving = [
-            (1, x_late[:, 0, :], late_plane[:, 0:S]),
-            (2, x_late[:, 1, :], late_plane[:, S:2 * S]),
+            (1, x_picked[2][:], late_plane[:, 0:S]),
+            (2, x_picked[3][:], late_plane[:, S:2 * S]),
             (0, z_codes[:], z_plane[:]),
         ]
         h2 = []
         for i in range(TILES):
-            if i == 2:
-                d_picked = pick_codewords(1)
             acc = psum.tile([P, S], F32, name="h_acc%d" % i)
             for n, (a, codes, plane) in enumerate(moving):
                 nc.tensor.matmul_mx(
                     out=acc[:],
-                    lhsT=d_picked[:, a, (i % 2) * P:(i % 2 + 1) * P].bitcast(FP8X4),
+                    lhsT=d_picked[i // 2][:, a, (i % 2) * P:(i % 2 + 1) * P].bitcast(FP8X4),
                     lhsT_scale=late_plane[:, 2 * S + a * H + i * P:2 * S + a * H + (i + 1) * P],
                     rhs=codes.bitcast(FP8X4), rhs_scale=plane,
                     start=(n == 0), stop=(n == 2))

@@ -66,8 +66,6 @@ def tile_picked_dhhzmthpolarecpx_none_p_kernel(
 
         quarter = new("quarter", [P, 1], F32)
         nc.gpsimd.memset(quarter[:], 0.25)
-        warm = new("warm", [P, 1], F32)
-        nc.scalar.activation(warm[:], quarter[:], ACT.Sqrt, bias=quarter[:])
         x_byte_win = load_scale_rows("x_byte_win", x_scales, T)
         l_offs = load_list("offs", offs)
         l_hz = load_list("hz", hz)

@@ -30,8 +30,8 @@ def tile_picked_dhhzmthpolarecpx_none_p_kernel(
         keep = ctx.enter_context(tc.tile_pool(name="keep", bufs=1))
         psum = ctx.enter_context(tc.psum_pool(name="psum", bufs=1))
 
-        def new(name, shape, dtype):
-            return keep.tile(shape, dtype, name=name, align_bytes=64)
+        def new(name, shape, dtype, slot=None):
+            return keep.tile(shape, dtype, name=name, tag=slot or name, align_bytes=64)
 
         def load_list(name, src):
             lst = new("list_" + name, list(src.shape), U16)
@@ -54,8 +54,8 @@ def tile_picked_dhhzmthpolarecpx_none_p_kernel(
             nc.sync.dma_start(rows[:], w.rearrange("(p j) c -> p j c", j=PACK))
             return rows
 
-        def place_scales(name, picked, width, queue):
-            plane = new(name, [P, width], U8)
+        def place_scales(name, picked, width, queue, slot=None):
+            plane = new(name, [P, width], U8, slot)
             nc.vector.tensor_copy(plane[:].bitcast(I32), picked[:].bitcast(I32))
             for j in range(1, 4):
                 queue.dma_start(plane[j:P:32, :].bitcast(I32), picked[8 * j:P:32, :].bitcast(I32))
@@ -66,6 +66,8 @@ def tile_picked_dhhzmthpolarecpx_none_p_kernel(
 
         quarter = new("quarter", [P, 1], F32)
         nc.gpsimd.memset(quarter[:], 0.25)
+        warm = new("warm", [P, 1], F32)
+        nc.scalar.activation(warm[:], quarter[:], ACT.Sqrt, bias=quarter[:])
         x_byte_win = load_scale_rows("x_byte_win", x_scales, T)
         l_offs = load_list("offs", offs)
         l_hz = load_list("hz", hz)
@@ -96,9 +98,9 @@ def tile_picked_dhhzmthpolarecpx_none_p_kernel(
             words = new("x_picked%d" % a, [P, S], U32)
             gather_words(words[:], x_word_win, lst[:])
             x_picked.append(words)
-        late_bytes = new("late_bytes", [P, 2 * S + 3 * H], U8)
+        x2_bytes = new("x2_bytes", [P, 2 * S], U8)
         for a, lst in enumerate((l_two, l_hy)):
-            nc.vector.tensor_copy(late_bytes[:, a * S:(a + 1) * S], x_byte_win[:].indirect(lst[:]))
+            nc.vector.tensor_copy(x2_bytes[:, a * S:(a + 1) * S], x_byte_win[:].indirect(lst[:]))
 
         grouped = [keep.tile([P, PACK * H], BF16, name="w_grouped%d" % a, tag="w_grouped%d" % a, align_bytes=64) for a in range(2)]
         dst = [grouped[a][:].rearrange("p (t m j) -> p m j t", t=TILES, j=PACK) for a in range(2)]
@@ -131,41 +133,49 @@ def tile_picked_dhhzmthpolarecpx_none_p_kernel(
                 nc.vector.tensor_copy(y_t[:], acc[:])
             y.append(y_t)
 
-        z_grouped = new("z_grouped", [P, S, PACK], BF16)
         pairs = []
-        for t in range(TILES):
-            pair = new("pair%d" % t, [P, S], F32)
-            nc.scalar.activation(pair[:, :W], y[t][:].indirect(l1[:]), ACT.Copy)
-            nc.scalar.activation(pair[:, W:], y[t][:].indirect(l2[:]), ACT.Copy)
+        for u in range(2):
+            pair = new("pair%d" % u, [P, 2, 2 * W], F32)
+            for e in range(2):
+                for side, lst in enumerate((l1, l2)):
+                    nc.scalar.activation(pair[:, side, e * W:(e + 1) * W], y[2 * u + e][:].indirect(lst[:]), ACT.Copy)
             pairs.append(pair)
-        for t in range(TILES):
-            pair = pairs[t]
-            rb = new("rb%d" % t, [P, W], F32)
-            sq = new("sq%d" % t, [P, S], F32)
-            ssum = new("ssum%d" % t, [P, W], F32)
-            ra = new("ra%d" % t, [P, W], F32)
-            ub = new("ub%d" % t, [P, S], F32)
-            nc.gpsimd.tensor_scalar(ssum[:], pair[:, :W], -0.5, 0.0, ALU.mult, ALU.add)
-            nc.gpsimd.tensor_tensor(rb[:], ssum[:], pair[:, W:], ALU.add)
+        ubs = []
+        for u in range(2):
+            pair = pairs[u]
+            rb = new("rb%d" % u, [P, 2 * W], F32)
+            neg_half = new("neg_half%d" % u, [P, 2 * W], F32)
+            sq = new("sq%d" % u, [P, 2, 2 * W], F32, "neg_half%d" % u)
+            ssum = new("ssum%d" % u, [P, 2 * W], F32)
+            ra = new("ra%d" % u, [P, 2 * W], F32)
+            nc.gpsimd.tensor_scalar(neg_half[:], pair[:, 0, :], -0.5, 0.0, ALU.mult, ALU.add)
+            nc.gpsimd.tensor_tensor(rb[:], neg_half[:], pair[:, 1, :], ALU.add)
             nc.gpsimd.tensor_tensor(sq[:], pair[:], pair[:], ALU.mult)
-            nc.gpsimd.tensor_tensor(ssum[:], sq[:, :W], sq[:, W:], ALU.add)
-            nc.scalar.activation(ub[:].indirect(l2[:]), rb[:], ACT.Copy)
+            nc.gpsimd.tensor_tensor(ssum[:], sq[:, 0, :], sq[:, 1, :], ALU.add)
+            ub = [new("ub%d" % (2 * u + e), [P, S], F32) for e in range(2)]
+            for e in range(2):
+                nc.scalar.activation(ub[e][:].indirect(l2[:]), rb[:, e * W:(e + 1) * W], ACT.Copy)
             nc.scalar.activation(ra[:], ssum[:], ACT.Sqrt, bias=quarter[:])
-            nc.scalar.activation(ub[:].indirect(l1[:]), ra[:], ACT.Copy)
-            nc.vector.tensor_scalar(z_grouped[:, :, t], ub[:], gain[:, t:t + 1], None, ALU.mult)
+            for e in range(2):
+                nc.scalar.activation(ub[e][:].indirect(l1[:]), ra[:, e * W:(e + 1) * W], ACT.Copy)
+            ubs.extend(ub)
 
+        x2_plane = place_scales("x2_plane", x2_bytes, 2 * S, nc.sync, "w_plane1")
+        d_bytes = new("d_bytes", [P, 3 * H], U8, "w_codes1")
         for a, lst in enumerate(d_lists):
-            at = 2 * S + a * H
-            nc.vector.tensor_copy(late_bytes[:, at:at + H], d_byte_win[:].indirect(lst[:]))
-        late_plane = place_scales("late_plane", late_bytes, 2 * S + 3 * H, nc.sync)
+            nc.vector.tensor_copy(d_bytes[:, a * H:(a + 1) * H], d_byte_win[:].indirect(lst[:]))
+        d_plane = place_scales("d_plane", d_bytes, 3 * H, nc.sync)
 
         def pick_codewords(h):
-            words = keep.tile([P, 3, S], U32, name="d_picked%d" % h, align_bytes=64)
-            for a, lst in enumerate(d_lists):
-                gather_words(words[:, a, :], d_word_win, lst[:, 16 * h:16 * (h + 1)])
+            words = new("d_picked%d" % h, [P, 3, S], U32, ("w_codes0", "sg1")[h])
+            for a in (1, 2, 0):
+                gather_words(words[:, a, :], d_word_win, d_lists[a][:, 16 * h:16 * (h + 1)])
             return words
 
-        d_picked = [pick_codewords(h) for h in range(2)]
+        d_picked = pick_codewords(0)
+        z_grouped = new("z_grouped", [P, S, PACK], BF16, "d_byte_win")
+        for t in range(TILES):
+            nc.vector.tensor_scalar(z_grouped[:, :, t], ubs[t][:], gain[:, t:t + 1], None, ALU.mult)
         z_codes = new("z_codes", [P, S], U32)
         z_plane = new("z_plane", [P, S], U8)
         nc.vector.quantize_mx(out=z_codes[:].bitcast(FP8X4), scales=z_plane[:], in_=z_grouped[:].rearrange("p c t -> p (c t)"))
@@ -173,38 +183,40 @@ def tile_picked_dhhzmthpolarecpx_none_p_kernel(
         nc.vector.scalar_tensor_tensor(bias[:], slope[:], -1.0, thresh[:], ALU.mult, ALU.mult)
 
         moving = [
-            (1, x_picked[2][:], late_plane[:, 0:S]),
-            (2, x_picked[3][:], late_plane[:, S:2 * S]),
+            (1, x_picked[2][:], x2_plane[:, 0:S]),
+            (2, x_picked[3][:], x2_plane[:, S:2 * S]),
             (0, z_codes[:], z_plane[:]),
         ]
-        h2 = []
-        for i in range(TILES):
-            acc = psum.tile([P, S], F32, name="h_acc%d" % i)
-            for n, (a, codes, plane) in enumerate(moving):
-                nc.tensor.matmul_mx(
-                    out=acc[:],
-                    lhsT=d_picked[i // 2][:, a, (i % 2) * P:(i % 2 + 1) * P].bitcast(FP8X4),
-                    lhsT_scale=late_plane[:, 2 * S + a * H + i * P:2 * S + a * H + (i + 1) * P],
-                    rhs=codes.bitcast(FP8X4), rhs_scale=plane,
-                    start=(n == 0), stop=(n == 2))
-            h_i = new("h%d" % i, [P, S], F32)
-            nc.vector.tensor_scalar(h_i[:], acc[:], 0.0625, None, ALU.mult)
-            h2.append(h_i)
-        for i in range(TILES):
-            sg = new("sg%d" % i, [P, S], F32)
-            st = new("st%d" % i, [P, S], F32)
-            pair = new("pair2_%d" % i, [P, S], F32)
-            big = new("big%d" % i, [P, W], F32)
-            diff = new("diff%d" % i, [P, W], F32)
-            res = new("res%d" % i, [P, S], F32)
-            for h in range(2):
-                nc.scalar.activation(sg[:, h * W:(h + 1) * W], h2[i][:].indirect(l3[:, 8 * h:8 * (h + 1)]), ACT.Sigmoid,
-                                     bias=bias[:, i:i + 1], scale=slope[:, i:i + 1])
-            nc.vector.tensor_tensor(st[:], h2[i][:], sg[:], ALU.mult)
-            nc.scalar.activation(pair[:, :W], st[:].indirect(l4[:]), ACT.Copy)
-            nc.scalar.activation(pair[:, W:], st[:].indirect(l5[:]), ACT.Copy)
-            nc.vector.tensor_tensor(big[:], pair[:, :W], pair[:, W:], ALU.max)
-            nc.vector.tensor_tensor(diff[:], pair[:, :W], pair[:, W:], ALU.subtract)
-            nc.scalar.activation(res[:].indirect(l6[:]), big[:], ACT.Copy)
-            nc.scalar.activation(res[:].indirect(l7[:]), diff[:], ACT.Copy)
-            nc.sync.dma_start(out[i * P:(i + 1) * P, :], res[:])
+        for half in range(2):
+            if half == 1:
+                d_picked = pick_codewords(1)
+            h2 = {}
+            for i in (2 * half, 2 * half + 1):
+                acc = psum.tile([P, S], F32, name="h_acc%d" % i)
+                for n, (a, codes, plane) in enumerate(moving):
+                    nc.tensor.matmul_mx(
+                        out=acc[:],
+                        lhsT=d_picked[:, a, (i % 2) * P:(i % 2 + 1) * P].bitcast(FP8X4),
+                        lhsT_scale=d_plane[:, a * H + i * P:a * H + (i + 1) * P],
+                        rhs=codes.bitcast(FP8X4), rhs_scale=plane,
+                        start=(n == 0), stop=(n == 2))
+                h2[i] = new("h%d" % i, [P, S], F32)
+                nc.vector.tensor_scalar(h2[i][:], acc[:], 0.0625, None, ALU.mult)
+            for i in (2 * half, 2 * half + 1):
+                sg = new("sg%d" % i, [P, S], F32)
+                st = new("st%d" % i, [P, S], F32)
+                pair = new("pair2_%d" % i, [P, S], F32)
+                big = new("big%d" % i, [P, W], F32)
+                diff = new("diff%d" % i, [P, W], F32)
+                res = new("res%d" % i, [P, S], F32)
+                for h in range(2):
+                    nc.scalar.activation(sg[:, h * W:(h + 1) * W], h2[i][:].indirect(l3[:, 8 * h:8 * (h + 1)]), ACT.Sigmoid,
+                                         bias=bias[:, i:i + 1], scale=slope[:, i:i + 1])
+                nc.vector.tensor_tensor(st[:], h2[i][:], sg[:], ALU.mult)
+                nc.scalar.activation(pair[:, :W], st[:].indirect(l4[:]), ACT.Copy)
+                nc.scalar.activation(pair[:, W:], st[:].indirect(l5[:]), ACT.Copy)
+                nc.vector.tensor_tensor(big[:], pair[:, :W], pair[:, W:], ALU.max)
+                nc.vector.tensor_tensor(diff[:], pair[:, :W], pair[:, W:], ALU.subtract)
+                nc.scalar.activation(res[:].indirect(l6[:]), big[:], ACT.Copy)
+                nc.scalar.activation(res[:].indirect(l7[:]), diff[:], ACT.Copy)
+                nc.sync.dma_start(out[i * P:(i + 1) * P, :], res[:])

from contextlib import ExitStack

import concourse.mybir as mybir

K, T, S, H, W, G = 512, 1024, 256, 512, 128, 2048
FLOPS = 5 * 2 * K * H * S

F32 = mybir.dt.float32
BF16 = mybir.dt.bfloat16
I32 = mybir.dt.int32
U32 = mybir.dt.uint32
U16 = mybir.dt.uint16
U8 = mybir.dt.uint8
FP8X4 = mybir.dt.float8_e4m3fn_x4
ALU = mybir.AluOpType
ACT = mybir.ActivationFunctionType

P = 128
PACK = 4
TILES = H // P
SPLIT = (32, 72)


def tile_picked_dhhzmthpolarecpx_none_p_kernel(
    tc, x_words, x_scales, w1, w2, gs, d_words, d_scales, sl, th,
    offs, hz, n1, n2, k1, k2, two, k3, hy, n3, n4, n5, n6, n7, out,
):
    nc = tc.nc
    with ExitStack() as ctx:
        keep = ctx.enter_context(tc.tile_pool(name="keep", bufs=1))
        psum = ctx.enter_context(tc.psum_pool(name="psum", bufs=1))

        def new(name, shape, dtype, slot=None):
            return keep.tile(shape, dtype, name=name, tag=slot or name, align_bytes=64)

        def load_list(name, src):
            lst = new("list_" + name, list(src.shape), U16)
            nc.sync.dma_start(lst[:], src)
            return lst

        def load_scale_rows(name, scales, width):
            window = new(name, [P, width], U8)
            rows = scales[0].bitcast(I32).unsqueeze(1).broadcast_to([16, 8, width // 4])
            nc.sync.dma_start(window[:].bitcast(I32), rows)
            return window

        def load_words(name, words, width):
            window = new(name, [P, width], I32)
            nc.sync.dma_start(window[:], words[0].rearrange("p n t -> p (n t)").bitcast(I32))
            return window

        def load_weight(name, w):
            rows = new(name, [P, PACK, H], F32)
            nc.sync.dma_start(rows[:], w.rearrange("(p j) c -> p j c", j=PACK))
            return rows

        def place_scales(name, picked, width, queue, slot=None):
            plane = new(name, [P, width], U8, slot)
            nc.vector.tensor_copy(plane[:].bitcast(I32), picked[:].bitcast(I32))
            for j in range(1, 4):
                queue.dma_start(plane[j:P:32, :].bitcast(I32), picked[8 * j:P:32, :].bitcast(I32))
            return plane

        def gather_words(dst, window, offsets):
            nc.vector.tensor_copy(dst, window[:].bitcast(U32).indirect(offsets))

        quarter = new("quarter", [P, 1], F32)
        nc.gpsimd.memset(quarter[:], 0.25)
        warm = new("warm", [P, 1], F32)
        nc.scalar.activation(warm[:], quarter[:], ACT.Sqrt, bias=quarter[:])
        x_byte_win = load_scale_rows("x_byte_win", x_scales, T)
        l_offs = load_list("offs", offs)
        l_hz = load_list("hz", hz)
        l_two = load_list("two", two)
        l_hy = load_list("hy", hy)
        x_word_win = load_words("x_word_win", x_words, T)
        raw = [load_weight("w1_raw", w1), load_weight("w2_raw", w2)]
        l1 = load_list("n1", n1)
        l2 = load_list("n2", n2)
        d_byte_win = load_scale_rows("d_byte_win", d_scales, G)
        d_lists = [load_list(name, src) for name, src in (("k1", k1), ("k2", k2), ("k3", k3))]
        d_word_win = load_words("d_word_win", d_words, G)
        gain = new("gain", [P, PACK], F32)
        nc.sync.dma_start(gain[:], gs.rearrange("(p t) o -> p (t o)", t=PACK))
        l3, l4, l5, l6, l7 = [load_list(name, src) for name, src in (("n3", n3), ("n4", n4), ("n5", n5), ("n6", n6), ("n7", n7))]
        slope = new("slope", [P, TILES], F32)
        thresh = new("thresh", [P, TILES], F32)
        with nc.allow_non_contiguous_dma(reason="one value a row"):
            nc.sync.dma_start(slope[:], sl.rearrange("(i p) o -> p (i o)", p=P))
            nc.sync.dma_start(thresh[:], th.rearrange("(i p) o -> p (i o)", p=P))

        x_bytes = new("x_bytes", [P, 2 * S], U8)
        for a, lst in enumerate((l_offs, l_hz)):
            nc.vector.tensor_copy(x_bytes[:, a * S:(a + 1) * S], x_byte_win[:].indirect(lst[:]))
        x_plane = place_scales("x_plane", x_bytes, 2 * S, nc.scalar)
        x_picked = []
        for a, lst in enumerate((l_offs, l_hz, l_two, l_hy)):
            words = new("x_picked%d" % a, [P, S], U32)
            gather_words(words[:], x_word_win, lst[:])
            x_picked.append(words)
        x2_bytes = new("x2_bytes", [P, 2 * S], U8)
        for a, lst in enumerate((l_two, l_hy)):
            nc.vector.tensor_copy(x2_bytes[:, a * S:(a + 1) * S], x_byte_win[:].indirect(lst[:]))

        grouped = [keep.tile([P, PACK * H], BF16, name="w_grouped%d" % a, tag="w_grouped%d" % a, align_bytes=64) for a in range(2)]
        dst = [grouped[a][:].rearrange("p (t m j) -> p m j t", t=TILES, j=PACK) for a in range(2)]
        src = [raw[a][:].rearrange("p j (m t) -> p m j t", t=TILES) for a in range(2)]
        for a in range(2):
            nc.vector.tensor_copy(dst[a][:, :SPLIT[a]], src[a][:, :SPLIT[a]])
            nc.scalar.copy(dst[a][:, SPLIT[a]:], src[a][:, SPLIT[a]:])
        w_codes = [new("w_codes%d" % a, [P, H], U32) for a in range(2)]
        w_plane = [new("w_plane%d" % a, [P, H], U8) for a in range(2)]

        y = []
        for t in range(TILES):
            cols = slice(t * P, (t + 1) * P)
            acc = psum.tile([P, S], F32, name="y_acc%d" % t)
            if t < 3:
                lo, hi = t * P, (t + 1) * P if t < 2 else H
                for a in range(2):
                    nc.vector.quantize_mx(
                        out=w_codes[a][:, lo:hi].bitcast(FP8X4), scales=w_plane[a][:, lo:hi],
                        in_=grouped[a][:, PACK * lo:PACK * hi])
            for a in range(2):
                nc.tensor.matmul_mx(
                    out=acc[:], lhsT=w_codes[a][:, cols].bitcast(FP8X4), lhsT_scale=w_plane[a][:, cols],
                    rhs=x_picked[a][:].bitcast(FP8X4), rhs_scale=x_plane[:, a * S:(a + 1) * S],
                    start=(a == 0), stop=(a == 1))
            y_t = new("y%d" % t, [P, S], F32)
            if t == 0:
                nc.scalar.copy(y_t[:], acc[:])
            else:
                nc.vector.tensor_copy(y_t[:], acc[:])
            y.append(y_t)

        pairs = []
        for u in range(2):
            pair = new("pair%d" % u, [P, 2, 2 * W], F32)
            for e in range(2):
                for side, lst in enumerate((l1, l2)):
                    nc.scalar.activation(pair[:, side, e * W:(e + 1) * W], y[2 * u + e][:].indirect(lst[:]), ACT.Copy)
            pairs.append(pair)
        ubs = []
        for u in range(2):
            pair = pairs[u]
            rb = new("rb%d" % u, [P, 2 * W], F32)
            neg_half = new("neg_half%d" % u, [P, 2 * W], F32)
            sq = new("sq%d" % u, [P, 2, 2 * W], F32, "neg_half%d" % u)
            ssum = new("ssum%d" % u, [P, 2 * W], F32)
            ra = new("ra%d" % u, [P, 2 * W], F32)
            nc.gpsimd.tensor_scalar(neg_half[:], pair[:, 0, :], -0.5, 0.0, ALU.mult, ALU.add)
            nc.gpsimd.tensor_tensor(rb[:], neg_half[:], pair[:, 1, :], ALU.add)
            nc.gpsimd.tensor_tensor(sq[:], pair[:], pair[:], ALU.mult)
            nc.gpsimd.tensor_tensor(ssum[:], sq[:, 0, :], sq[:, 1, :], ALU.add)
            ub = [new("ub%d" % (2 * u + e), [P, S], F32) for e in range(2)]
            for e in range(2):
                nc.scalar.activation(ub[e][:].indirect(l2[:]), rb[:, e * W:(e + 1) * W], ACT.Copy)
            nc.scalar.activation(ra[:], ssum[:], ACT.Sqrt, bias=quarter[:])
            for e in range(2):
                nc.scalar.activation(ub[e][:].indirect(l1[:]), ra[:, e * W:(e + 1) * W], ACT.Copy)
            ubs.extend(ub)

        x2_plane = place_scales("x2_plane", x2_bytes, 2 * S, nc.sync, "w_plane1")
        d_bytes = new("d_bytes", [P, 3 * H], U8, "w_codes1")
        for a, lst in enumerate(d_lists):
            nc.vector.tensor_copy(d_bytes[:, a * H:(a + 1) * H], d_byte_win[:].indirect(lst[:]))
        d_plane = place_scales("d_plane", d_bytes, 3 * H, nc.sync)

        def pick_codewords(h):
            words = new("d_picked%d" % h, [P, 3, S], U32, ("w_codes0", "sg1")[h])
            for a in (1, 2, 0):
                gather_words(words[:, a, :], d_word_win, d_lists[a][:, 16 * h:16 * (h + 1)])
            return words

        d_picked = pick_codewords(0)
        z_grouped = new("z_grouped", [P, S, PACK], BF16, "d_byte_win")
        for t in range(TILES):
            nc.vector.tensor_scalar(z_grouped[:, :, t], ubs[t][:], gain[:, t:t + 1], None, ALU.mult)
        z_codes = new("z_codes", [P, S], U32)
        z_plane = new("z_plane", [P, S], U8)
        nc.vector.quantize_mx(out=z_codes[:].bitcast(FP8X4), scales=z_plane[:], in_=z_grouped[:].rearrange("p c t -> p (c t)"))
        bias = new("bias", [P, TILES], F32)
        nc.vector.scalar_tensor_tensor(bias[:], slope[:], -1.0, thresh[:], ALU.mult, ALU.mult)

        moving = [
            (1, x_picked[2][:], x2_plane[:, 0:S]),
            (2, x_picked[3][:], x2_plane[:, S:2 * S]),
            (0, z_codes[:], z_plane[:]),
        ]
        for half in range(2):
            if half == 1:
                d_picked = pick_codewords(1)
            h2 = {}
            for i in (2 * half, 2 * half + 1):
                acc = psum.tile([P, S], F32, name="h_acc%d" % i)
                for n, (a, codes, plane) in enumerate(moving):
                    nc.tensor.matmul_mx(
                        out=acc[:],
                        lhsT=d_picked[:, a, (i % 2) * P:(i % 2 + 1) * P].bitcast(FP8X4),
                        lhsT_scale=d_plane[:, a * H + i * P:a * H + (i + 1) * P],
                        rhs=codes.bitcast(FP8X4), rhs_scale=plane,
                        start=(n == 0), stop=(n == 2))
                h2[i] = new("h%d" % i, [P, S], F32)
                nc.vector.tensor_scalar(h2[i][:], acc[:], 0.0625, None, ALU.mult)
            for i in (2 * half, 2 * half + 1):
                sg = new("sg%d" % i, [P, S], F32)
                st = new("st%d" % i, [P, S], F32)
                pair = new("pair2_%d" % i, [P, S], F32)
                big = new("big%d" % i, [P, W], F32)
                diff = new("diff%d" % i, [P, W], F32)
                res = new("res%d" % i, [P, S], F32)
                for h in range(2):
                    nc.scalar.activation(sg[:, h * W:(h + 1) * W], h2[i][:].indirect(l3[:, 8 * h:8 * (h + 1)]), ACT.Sigmoid,
                                         bias=bias[:, i:i + 1], scale=slope[:, i:i + 1])
                nc.vector.tensor_tensor(st[:], h2[i][:], sg[:], ALU.mult)
                nc.scalar.activation(pair[:, :W], st[:].indirect(l4[:]), ACT.Copy)
                nc.scalar.activation(pair[:, W:], st[:].indirect(l5[:]), ACT.Copy)
                nc.vector.tensor_tensor(big[:], pair[:, :W], pair[:, W:], ALU.max)
                nc.vector.tensor_tensor(diff[:], pair[:, :W], pair[:, W:], ALU.subtract)
                nc.scalar.activation(res[:].indirect(l6[:]), big[:], ACT.Copy)
                nc.scalar.activation(res[:].indirect(l7[:]), diff[:], ACT.Copy)
                nc.sync.dma_start(out[i * P:(i + 1) * P, :], res[:])
